import numpy as np
import ml_dtypes


def mxq(x, axis, fmt="e4m3"):
    dtype, down = {"e4m3": (ml_dtypes.float8_e4m3fn, 7), "e5m2": (ml_dtypes.float8_e5m2, 14)}[fmt]
    v = np.moveaxis(np.asarray(x, np.float32).astype(ml_dtypes.bfloat16).astype(np.float64), axis, -1)
    blocks = v.reshape(v.shape[:-1] + (-1, 32))
    amax = np.abs(blocks).max(-1, keepdims=True)
    byte = np.maximum(np.where(amax > 0, np.frexp(amax)[1] - 1 + 127, 0) - down, 1)
    scale = np.exp2(byte - 127.0)
    codes = (blocks / scale).astype(np.float32).astype(dtype).astype(np.float64)
    return np.moveaxis((codes * scale).reshape(v.shape), -1, axis)


WIDE = False


def mx_kscale(k):
    if not WIDE:
        return np.ones(k)
    levels = np.array([10, -10, 5, -5, 0])
    if k % 512:
        return np.exp2(np.random.permutation(np.resize(levels, k // 32))).repeat(32)
    a = np.empty((k // 512, 16))
    for p in range(k // 512):
        a[p, :8] = np.random.permutation(np.resize(levels, 8))
        for g in range(8):
            far = levels[np.abs(levels - a[p, g]) >= 10]
            a[p, g + 8] = far[np.random.randint(len(far))]
    return np.exp2(a.ravel()).repeat(32)


def f64(x):
    return np.asarray(x).astype(np.float64)


def striped8(idx):
    return np.concatenate([x.reshape(-1, 16).T for x in idx]).astype(np.uint16)


def runs(offs, k):
    lists = np.stack([offs[16 * r : 16 * r + 16].T.reshape(-1) for r in range(8)]).astype(np.int64)
    return lists[np.arange(k) % 512 // 64]


def pack_weight(w):
    k, n = w.shape
    w = f64(np.asarray(w, np.float32).astype(ml_dtypes.bfloat16)).reshape(k // 32, 32, n)
    amax = np.abs(w).max(1)
    byte = np.clip(np.where(amax > 0, np.frexp(amax)[1] - 1 + 127 - 7, 1), 1, 254)
    scaled = (w * np.exp2(127.0 - byte)[:, None, :]).reshape(k, n).astype(np.float32)
    words = np.ascontiguousarray(scaled.reshape(k // 512, 128, 4, n).transpose(0, 1, 3, 2)).astype(ml_dtypes.float8_e4m3fn).view(np.uint8)
    return words, np.ascontiguousarray(byte.astype(np.uint8).reshape(k // 512, 16, n))


def unpack_weight(words, scales):
    g, p, n, _ = words.shape
    vals = np.ascontiguousarray(words).view(ml_dtypes.float8_e4m3fn).astype(np.float64) * np.repeat(np.exp2(scales.astype(np.float64) - 127.0), 8, axis=1)[..., None]
    return vals.transpose(0, 1, 3, 2).reshape(g * 512, n)


E2M1 = np.array([0.0, 0.5, 1.0, 1.5, 2.0, 3.0, 4.0, 6.0, -0.0, -0.5, -1.0, -1.5, -2.0, -3.0, -4.0, -6.0])


def pack_fp4(w):
    k, n = w.shape
    w = f64(np.asarray(w, np.float32).astype(ml_dtypes.bfloat16)).reshape(k // 32, 32, n)
    amax = np.abs(w).max(1)
    mant, ex = np.frexp(amax / 6.0)
    byte = np.clip(np.where(amax > 0, np.where(mant > 0.5, ex, ex - 1) + 127, 1), 1, 254)
    scaled = (w * np.exp2(127.0 - byte)[:, None, :]).reshape(k, n).astype(np.float32)
    c = np.ascontiguousarray(scaled.reshape(k // 512, 128, 4, n).transpose(0, 1, 3, 2)).astype(ml_dtypes.float4_e2m1fn).view(np.uint8) & 0xF
    words = (c[..., 0::2] | (c[..., 1::2] << 4)).reshape(k // 512, 128, 2 * n)
    return np.ascontiguousarray(words), np.ascontiguousarray(byte.astype(np.uint8).reshape(k // 512, 16, n))


def unpack_fp4(words, scales):
    g, _, n = scales.shape
    words = np.ascontiguousarray(words).reshape(g, 128, n, 2)
    nib = np.empty((g, 128, n, 4), np.uint8)
    nib[..., 0::2] = words & 0xF
    nib[..., 1::2] = words >> 4
    vals = E2M1[nib] * np.repeat(np.exp2(scales.astype(np.float64) - 127.0), 8, axis=1)[..., None]
    return vals.transpose(0, 1, 3, 2).reshape(g * 512, n)


def relu(v):
    return np.maximum(v, 0.0)

def planes(y):
    n, m = y.shape
    v = y.astype(np.float32).astype(ml_dtypes.bfloat16).astype(np.float64).reshape(n // 32, 32, m)
    top = np.abs(v).max(1)
    byte = np.clip(np.where(top > 0, np.frexp(top)[1] - 1 + 127 - 7, 1), 1, 254)
    codes = (v * np.exp2(127.0 - byte)[:, None, :]).reshape(n, m).astype(np.float32).astype(ml_dtypes.float8_e4m3fn).view(np.uint8)
    words = codes.reshape(n // 512, 128, 4, m).transpose(0, 1, 3, 2)
    return np.ascontiguousarray(words), np.ascontiguousarray(byte.astype(np.uint8).reshape(n // 512, 16, m))


K, T, S, N, H = 512, 2048, 512, 512, 512


def setup_inputs():
    n = np.random.standard_normal
    s = mx_kscale(K)[:, None]
    u = mx_kscale(H)
    packed_xT = pack_weight(n((K, T)) * s)
    packed_w1 = pack_fp4(n((K, H)) / np.sqrt(K) / s)
    packed_w2 = pack_fp4(n((H, N)) / np.sqrt(H) / u[:, None])
    return {
        "x_words": packed_xT[0],
        "x_scales": packed_xT[1],
        "w1_words": packed_w1[0],
        "w1_scales": packed_w1[1],
        "gn": (np.random.uniform(0.5, 1.5, (H, 1)) * u[:, None]).astype(np.float32),
        "w2_words": packed_w2[0],
        "w2_scales": packed_w2[1],
        "offs": striped8(np.random.randint(0, T, (8, S))),
        "n1": striped8(np.stack([np.random.permutation(S) for _ in range(8)])),
        "n2": striped8(np.stack([np.random.permutation(S) for _ in range(8)])),
        "n3": striped8(np.stack([np.random.permutation(S) for _ in range(8)])),
        "n4": striped8(np.stack([np.random.permutation(S) for _ in range(8)])),
    }


def reference(x_words, x_scales, w1_words, w1_scales, gn, w2_words, w2_scales, offs, n1, n2, n3, n4):
    xq = unpack_weight(x_words, x_scales)[np.arange(K)[:, None], runs(offs, K)]
    y = unpack_fp4(w1_words, w1_scales).T @ xq
    z = f64(gn) * (y[np.arange(H)[:, None], runs(n1, H)] - (y[np.arange(H)[:, None], runs(n2, H)]))
    h = unpack_fp4(w2_words, w2_scales).T @ mxq(z, 0, "e4m3")
    out_0 = relu(h - (h[np.arange(N)[:, None], runs(n3, N)])) + 0.5 * (relu(h[np.arange(N)[:, None], runs(n4, N)] - h))
    return (out_0,) + planes(out_0)

@@ -1,0 +1,166 @@
+from contextlib import ExitStack
+
+import concourse.mybir as mybir
+
+K, T, S, H, N = 512, 2048, 512, 512, 512
+FLOPS = 2 * K * H * S + 2 * H * N * S
+
+F32 = mybir.dt.float32
+BF16 = mybir.dt.bfloat16
+I32 = mybir.dt.int32
+U32 = mybir.dt.uint32
+U16 = mybir.dt.uint16
+U8 = mybir.dt.uint8
+FP8X4 = mybir.dt.float8_e4m3fn_x4
+FP4X4 = mybir.dt.float4_e2m1fn_x4
+ALU = mybir.AluOpType
+ACT = mybir.ActivationFunctionType
+
+P = 128
+PACK = 4
+HALVES = [(0, 256), (256, 256)]
+CHUNKS = [(0, 256), (256, 128), (384, 128)]
+
+
+def tile_picked_hashgaphinge_none_po_kernel(
+    tc, x_words, x_scales, w1_words, w1_scales, gn, w2_words, w2_scales, offs, n1, n2, n3, n4, out_0, out_1, out_2
+):
+    nc = tc.nc
+    with ExitStack() as ctx:
+        pool = ctx.enter_context(tc.tile_pool(name="pool", bufs=1))
+        psum = ctx.enter_context(tc.psum_pool(name="psum", bufs=1))
+
+        def sb(name, shape, dtype):
+            return pool.tile(shape, dtype, name=name, align_bytes=64)
+
+        def bank(index, name):
+            return psum.tile([P, 512], F32, name=name, tag="bank%d" % index)
+
+        def cut(lists, j0, n):
+            return lists[:, j0 // 16 : (j0 + n) // 16]
+
+        lists = [sb(name, [P, S // 16], U16) for name in ("offs_t", "n1_t", "n2_t", "n3_t", "n4_t")]
+        offs_t, n1_t, n2_t, n3_t, n4_t = lists
+        xw = sb("xw", [P, T], U32)
+        xs = sb("xs", [P, T], U8)
+        xs_g = sb("xs_g", [P, S], U8)
+        xs_p = sb("xs_p", [P, S], U8)
+        ww_raw = sb("ww_raw", [P, 2 * H], U8)
+        ws_raw = sb("ws_raw", [P, H], U8)
+        gain = sb("gain", [P, PACK], F32)
+        warm = sb("warm", [P, 1], F32)
+        warm_out = sb("warm_out", [P, 1], F32)
+
+        nc.vector.memset(xs[:].bitcast(I32), 0)
+        nc.gpsimd.memset(ws_raw[:].bitcast(I32), 0)
+        nc.vector.memset(warm[:], 0.0)
+        nc.vector.memset(xs_p[:].bitcast(I32), 0)
+
+        for tile, src in zip(lists, (offs, n1, n2, n3, n4)):
+            nc.sync.dma_start(tile[:], src)
+        nc.sync.dma_start(xw[:].bitcast(I32), x_words[0].rearrange("p n t -> p (n t)").bitcast(I32))
+        nc.scalar.dma_start(ww_raw[:].bitcast(I32), w1_words[0].bitcast(I32))
+        nc.scalar.dma_start(xs[0:P:8, :].bitcast(I32), x_scales[0].bitcast(I32))
+        for q in range(4):
+            nc.gpsimd.dma_start(ws_raw[32 * q : 32 * q + 4, :].bitcast(I32), w1_scales[0, 4 * q : 4 * q + 4, :].bitcast(I32))
+        nc.gpsimd.dma_start(gain[:], gn.rearrange("(p t) o -> p (t o)", t=PACK))
+        nc.scalar.activation(warm_out[:], warm[:], ACT.Relu)
+
+        def deal_words(name):
+            dealt = sb(name, [P, 2 * H], U8)
+            nc.vector.tensor_copy(
+                out=dealt[:].rearrange("p (t m b) -> p t m b", t=PACK, b=2),
+                in_=ww_raw[:].rearrange("p (m t b) -> p t m b", t=PACK, b=2),
+            )
+            return dealt
+
+        def deal_scales(name):
+            dealt = sb(name, [P, H], U8)
+            nc.vector.tensor_copy(
+                out=dealt[:].rearrange("p (t m) -> p t m", t=PACK),
+                in_=ws_raw[:].rearrange("p (m t) -> p t m", t=PACK),
+            )
+            return dealt
+
+        nc.vector.tensor_copy(xs_g[:], xs[:].indirect(offs_t[:]))
+        for q in range(4):
+            nc.sync.dma_start(xs_p[32 * q : 32 * q + 4, :].bitcast(I32), xs_g[32 * q : 32 * q + 32 : 8, :].bitcast(I32))
+        w1w = deal_words("w1w")
+        nc.sync.dma_start(ww_raw[:].bitcast(I32), w2_words[0].bitcast(I32))
+        w1s = deal_scales("w1s")
+        for q in range(4):
+            nc.sync.dma_start(ws_raw[32 * q : 32 * q + 4, :].bitcast(I32), w2_scales[0, 4 * q : 4 * q + 4, :].bitcast(I32))
+
+        def product(out, words, scales, t, rhs, rhs_scale):
+            nc.tensor.matmul_mx(
+                out=out,
+                lhsT=words[:, 2 * P * t : 2 * P * (t + 1)].bitcast(FP4X4),
+                lhsT_scale=scales[:, P * t : P * (t + 1)],
+                rhs=rhs.bitcast(FP8X4),
+                rhs_scale=rhs_scale,
+                start=True,
+                stop=True,
+            )
+
+        y = [sb("y%d" % t, [P, S], F32) for t in range(PACK)]
+        for c, (j0, n) in enumerate(HALVES):
+            xq = sb("xq%d" % c, [P, n], U32)
+            nc.vector.tensor_copy(xq[:], xw[:].indirect(cut(offs_t, j0, n)))
+            for t in range(PACK):
+                acc = bank(4 * c + t, "y_acc%d_%d" % (c, t))
+                product(acc[:, :n], w1w, w1s, t, xq[:], xs_p[:, j0 : j0 + n])
+                nc.scalar.activation(y[t][:, j0 : j0 + n], acc[:, :n], ACT.Copy, scale=gain[:, t : t + 1])
+        w2w = deal_words("w2w")
+        w2s = deal_scales("w2s")
+
+        def quantise(name, values, n, last, words, scales):
+            grouped = sb(name, [P, n, PACK], BF16)
+            if last:
+                nc.vector.tensor_copy(out=grouped[:], in_=values[:].rearrange("p t j -> p j t"))
+            else:
+                nc.scalar.copy(out=grouped[:], in_=values[:].rearrange("p t j -> p j t"))
+            nc.vector.quantize_mx(out=words.bitcast(FP8X4), scales=scales, in_=grouped[:].rearrange("p j t -> p (j t)"))
+
+        h_pos = [sb("h_pos%d" % t, [P, S], F32) for t in range(PACK)]
+        h_neg = [sb("h_neg%d" % t, [P, S], F32) for t in range(PACK)]
+        for c, (j0, n) in enumerate(CHUNKS):
+            z = sb("z%d" % c, [P, PACK, n], F32)
+            sub = sb("sub%d" % c, [P, PACK, n], F32)
+            for t in range(PACK + 1):
+                if t < PACK:
+                    nc.vector.tensor_copy(sub[:, t, :], y[t][:].indirect(cut(n2_t, j0, n)))
+                if t > 0:
+                    nc.vector.tensor_tensor(z[:, t - 1, :], y[t - 1][:].indirect(cut(n1_t, j0, n)), sub[:, t - 1, :], ALU.subtract)
+            zw = sb("zw%d" % c, [P, n], U32)
+            zs = sb("zs%d" % c, [P, n], U8)
+            quantise("zb%d" % c, z, n, c == len(CHUNKS) - 1, zw[:], zs[:])
+            for t in range(PACK):
+                acc = bank(4 * (c % 2) + t, "h_acc%d_%d" % (c, t))
+                product(acc[:, :n], w2w, w2s, t, zw[:], zs[:])
+                nc.scalar.activation(h_pos[t][:, j0 : j0 + n], acc[:, :n], ACT.Copy)
+                nc.scalar.activation(h_neg[t][:, j0 : j0 + n], acc[:, :n], ACT.Copy, scale=-1.0)
+
+        out_rows = out_0.rearrange("(p t) j -> p t j", t=PACK)
+        out_words = out_1[0].rearrange("p j t -> p (j t)").bitcast(I32)
+        os_all = sb("os_all", [P, S], U8)
+        for c, (j0, n) in enumerate(CHUNKS):
+            up = sb("up%d" % c, [P, PACK, n], F32)
+            half_up = sb("half_up%d" % c, [P, PACK, n], F32)
+            down = sb("down%d" % c, [P, PACK, n], F32)
+            res = sb("res%d" % c, [P, PACK, n], F32)
+            for t in range(PACK + 1):
+                if t < PACK:
+                    nc.vector.tensor_tensor(up[:, t, :], h_pos[t][:].indirect(cut(n4_t, j0, n)), h_neg[t][:, j0 : j0 + n], ALU.add)
+                    nc.scalar.activation(half_up[:, t, :], up[:, t, :], ACT.Relu, scale=0.5)
+                    nc.vector.tensor_tensor(down[:, t, :], h_neg[t][:].indirect(cut(n3_t, j0, n)), h_pos[t][:, j0 : j0 + n], ALU.add)
+                if t > 0:
+                    nc.vector.scalar_tensor_tensor(
+                        out=res[:, t - 1, :], in0=down[:, t - 1, :], scalar=0.0, in1=half_up[:, t - 1, :], op0=ALU.max, op1=ALU.add
+                    )
+            ow = sb("ow%d" % c, [P, n], U32)
+            quantise("ob%d" % c, res, n, c == len(CHUNKS) - 1, ow[:], os_all[:, j0 : j0 + n])
+            nc.sync.dma_start(out_rows[:, :, j0 : j0 + n], res[:])
+            nc.sync.dma_start(out_words[:, j0 : j0 + n], ow[:].bitcast(I32))
+        for q in range(4):
+            queue = nc.scalar if q % 2 else nc.sync
+            queue.dma_start(out_2[0, 4 * q : 4 * q + 4, :].bitcast(I32), os_all[32 * q : 32 * q + 4, :].bitcast(I32))

@@ -30,8 +30,8 @@ def tile_picked_hashgaphinge_none_po_kernel(
         pool = ctx.enter_context(tc.tile_pool(name="pool", bufs=1))
         psum = ctx.enter_context(tc.psum_pool(name="psum", bufs=1))
 
-        def sb(name, shape, dtype):
-            return pool.tile(shape, dtype, name=name, align_bytes=64)
+        def sb(name, shape, dtype, tag=None, bufs=1):
+            return pool.tile(shape, dtype, name=name, tag=tag or name, bufs=bufs, align_bytes=64)
 
         def bank(index, name):
             return psum.tile([P, 512], F32, name=name, tag="bank%d" % index)
@@ -45,32 +45,35 @@ def tile_picked_hashgaphinge_none_po_kernel(
         xs = sb("xs", [P, T], U8)
         xs_g = sb("xs_g", [P, S], U8)
         xs_p = sb("xs_p", [P, S], U8)
-        ww_raw = sb("ww_raw", [P, 2 * H], U8)
+        w1_raw = sb("w1_raw", [P, 2 * H], U8)
+        w2_raw = sb("w2_raw", [P, 2 * N], U8)
         ws_raw = sb("ws_raw", [P, H], U8)
         gain = sb("gain", [P, PACK], F32)
         warm = sb("warm", [P, 1], F32)
         warm_out = sb("warm_out", [P, 1], F32)
 
-        nc.vector.memset(xs[:].bitcast(I32), 0)
+        nc.gpsimd.memset(xs[:].bitcast(I32), 0)
         nc.gpsimd.memset(ws_raw[:].bitcast(I32), 0)
-        nc.vector.memset(warm[:], 0.0)
         nc.vector.memset(xs_p[:].bitcast(I32), 0)
+        nc.gpsimd.memset(warm[:], 0.0)
 
-        for tile, src in zip(lists, (offs, n1, n2, n3, n4)):
+        for tile, src in ((offs_t, offs), (n2_t, n2), (n1_t, n1), (n4_t, n4), (n3_t, n3)):
             nc.sync.dma_start(tile[:], src)
         nc.sync.dma_start(xw[:].bitcast(I32), x_words[0].rearrange("p n t -> p (n t)").bitcast(I32))
-        nc.scalar.dma_start(ww_raw[:].bitcast(I32), w1_words[0].bitcast(I32))
         nc.scalar.dma_start(xs[0:P:8, :].bitcast(I32), x_scales[0].bitcast(I32))
+        nc.scalar.dma_start(w1_raw[:].bitcast(I32), w1_words[0].bitcast(I32))
         for q in range(4):
-            nc.gpsimd.dma_start(ws_raw[32 * q : 32 * q + 4, :].bitcast(I32), w1_scales[0, 4 * q : 4 * q + 4, :].bitcast(I32))
+            queue = nc.scalar if q < 2 else nc.gpsimd
+            queue.dma_start(ws_raw[32 * q : 32 * q + 4, :].bitcast(I32), w1_scales[0, 4 * q : 4 * q + 4, :].bitcast(I32))
         nc.gpsimd.dma_start(gain[:], gn.rearrange("(p t) o -> p (t o)", t=PACK))
+        nc.gpsimd.dma_start(w2_raw[:].bitcast(I32), w2_words[0].bitcast(I32))
         nc.scalar.activation(warm_out[:], warm[:], ACT.Relu)
 
-        def deal_words(name):
-            dealt = sb(name, [P, 2 * H], U8)
+        def deal_words(name, raw, tag=None):
+            dealt = sb(name, [P, 2 * H], U8, tag=tag)
             nc.vector.tensor_copy(
                 out=dealt[:].rearrange("p (t m b) -> p t m b", t=PACK, b=2),
-                in_=ww_raw[:].rearrange("p (m t b) -> p t m b", t=PACK, b=2),
+                in_=raw[:].rearrange("p (m t b) -> p t m b", t=PACK, b=2),
             )
             return dealt
 
@@ -84,9 +87,9 @@ def tile_picked_hashgaphinge_none_po_kernel(
 
         nc.vector.tensor_copy(xs_g[:], xs[:].indirect(offs_t[:]))
         for q in range(4):
-            nc.sync.dma_start(xs_p[32 * q : 32 * q + 4, :].bitcast(I32), xs_g[32 * q : 32 * q + 32 : 8, :].bitcast(I32))
-        w1w = deal_words("w1w")
-        nc.sync.dma_start(ww_raw[:].bitcast(I32), w2_words[0].bitcast(I32))
+            queue = nc.scalar if q % 2 else nc.sync
+            queue.dma_start(xs_p[32 * q : 32 * q + 4, :].bitcast(I32), xs_g[32 * q : 32 * q + 32 : 8, :].bitcast(I32))
+        w1w = deal_words("w1w", w1_raw)
         w1s = deal_scales("w1s")
         for q in range(4):
             nc.sync.dma_start(ws_raw[32 * q : 32 * q + 4, :].bitcast(I32), w2_scales[0, 4 * q : 4 * q + 4, :].bitcast(I32))
@@ -103,14 +106,16 @@ def tile_picked_hashgaphinge_none_po_kernel(
             )
 
         y = [sb("y%d" % t, [P, S], F32) for t in range(PACK)]
+        xq = []
         for c, (j0, n) in enumerate(HALVES):
-            xq = sb("xq%d" % c, [P, n], U32)
-            nc.vector.tensor_copy(xq[:], xw[:].indirect(cut(offs_t, j0, n)))
-            for t in range(PACK):
+            xq.append(sb("xq%d" % c, [P, n], U32))
+            nc.vector.tensor_copy(xq[c][:], xw[:].indirect(cut(offs_t, j0, n)))
+        for t in range(PACK):
+            for c, (j0, n) in enumerate(HALVES):
                 acc = bank(4 * c + t, "y_acc%d_%d" % (c, t))
-                product(acc[:, :n], w1w, w1s, t, xq[:], xs_p[:, j0 : j0 + n])
+                product(acc[:, :n], w1w, w1s, t, xq[c][:], xs_p[:, j0 : j0 + n])
                 nc.scalar.activation(y[t][:, j0 : j0 + n], acc[:, :n], ACT.Copy, scale=gain[:, t : t + 1])
-        w2w = deal_words("w2w")
+        w2w = deal_words("w2w", w2_raw, tag="xw")
         w2s = deal_scales("w2s")
 
         def quantise(name, values, n, last, words, scales):
@@ -124,13 +129,17 @@ def tile_picked_hashgaphinge_none_po_kernel(
         h_pos = [sb("h_pos%d" % t, [P, S], F32) for t in range(PACK)]
         h_neg = [sb("h_neg%d" % t, [P, S], F32) for t in range(PACK)]
         for c, (j0, n) in enumerate(CHUNKS):
-            z = sb("z%d" % c, [P, PACK, n], F32)
-            sub = sb("sub%d" % c, [P, PACK, n], F32)
+            z = sb("z%d" % c, [P, PACK, n], F32, tag="zb0" if c == 2 else None)
+            subs = []
             for t in range(PACK + 1):
                 if t < PACK:
-                    nc.vector.tensor_copy(sub[:, t, :], y[t][:].indirect(cut(n2_t, j0, n)))
+                    if (c, t) == (2, 2):
+                        subs.append(sb("sub%d_%d" % (c, t), [P, n], F32, tag="zb1"))
+                    else:
+                        subs.append(sb("sub%d_%d" % (c, t), [P, n], F32, tag="sub", bufs=2))
+                    nc.vector.tensor_copy(subs[t][:], y[t][:].indirect(cut(n2_t, j0, n)))
                 if t > 0:
-                    nc.vector.tensor_tensor(z[:, t - 1, :], y[t - 1][:].indirect(cut(n1_t, j0, n)), sub[:, t - 1, :], ALU.subtract)
+                    nc.vector.tensor_tensor(z[:, t - 1, :], y[t - 1][:].indirect(cut(n1_t, j0, n)), subs[t - 1][:], ALU.subtract)
             zw = sb("zw%d" % c, [P, n], U32)
             zs = sb("zs%d" % c, [P, n], U8)
             quantise("zb%d" % c, z, n, c == len(CHUNKS) - 1, zw[:], zs[:])
@@ -146,16 +155,17 @@ def tile_picked_hashgaphinge_none_po_kernel(
         for c, (j0, n) in enumerate(CHUNKS):
             up = sb("up%d" % c, [P, PACK, n], F32)
             half_up = sb("half_up%d" % c, [P, PACK, n], F32)
-            down = sb("down%d" % c, [P, PACK, n], F32)
+            downs = []
             res = sb("res%d" % c, [P, PACK, n], F32)
             for t in range(PACK + 1):
                 if t < PACK:
                     nc.vector.tensor_tensor(up[:, t, :], h_pos[t][:].indirect(cut(n4_t, j0, n)), h_neg[t][:, j0 : j0 + n], ALU.add)
                     nc.scalar.activation(half_up[:, t, :], up[:, t, :], ACT.Relu, scale=0.5)
-                    nc.vector.tensor_tensor(down[:, t, :], h_neg[t][:].indirect(cut(n3_t, j0, n)), h_pos[t][:, j0 : j0 + n], ALU.add)
+                    downs.append(sb("down%d_%d" % (c, t), [P, n], F32, tag="down", bufs=2))
+                    nc.vector.tensor_tensor(downs[t][:], h_neg[t][:].indirect(cut(n3_t, j0, n)), h_pos[t][:, j0 : j0 + n], ALU.add)
                 if t > 0:
                     nc.vector.scalar_tensor_tensor(
-                        out=res[:, t - 1, :], in0=down[:, t - 1, :], scalar=0.0, in1=half_up[:, t - 1, :], op0=ALU.max, op1=ALU.add
+                        out=res[:, t - 1, :], in0=downs[t - 1][:], scalar=0.0, in1=half_up[:, t - 1, :], op0=ALU.max, op1=ALU.add
                     )
             ow = sb("ow%d" % c, [P, n], U32)
             quantise("ob%d" % c, res, n, c == len(CHUNKS) - 1, ow[:], os_all[:, j0 : j0 + n])

@@ -52,19 +52,19 @@ def tile_picked_hashgaphinge_none_po_kernel(
         warm = sb("warm", [P, 1], F32)
         warm_out = sb("warm_out", [P, 1], F32)
 
-        nc.gpsimd.memset(xs[:].bitcast(I32), 0)
+        nc.vector.memset(xs[:].bitcast(I32), 0)
         nc.gpsimd.memset(ws_raw[:].bitcast(I32), 0)
-        nc.vector.memset(xs_p[:].bitcast(I32), 0)
+        nc.gpsimd.memset(xs_p[:].bitcast(I32), 0)
         nc.gpsimd.memset(warm[:], 0.0)
 
-        for tile, src in ((offs_t, offs), (n2_t, n2), (n1_t, n1), (n4_t, n4), (n3_t, n3)):
-            nc.sync.dma_start(tile[:], src)
+        nc.sync.dma_start(offs_t[:], offs)
+        nc.sync.dma_start(w1_raw[:].bitcast(I32), w1_words[0].bitcast(I32))
         nc.sync.dma_start(xw[:].bitcast(I32), x_words[0].rearrange("p n t -> p (n t)").bitcast(I32))
+        for tile, src in ((n2_t, n2), (n1_t, n1), (n4_t, n4), (n3_t, n3)):
+            nc.sync.dma_start(tile[:], src)
         nc.scalar.dma_start(xs[0:P:8, :].bitcast(I32), x_scales[0].bitcast(I32))
-        nc.scalar.dma_start(w1_raw[:].bitcast(I32), w1_words[0].bitcast(I32))
         for q in range(4):
-            queue = nc.scalar if q < 2 else nc.gpsimd
-            queue.dma_start(ws_raw[32 * q : 32 * q + 4, :].bitcast(I32), w1_scales[0, 4 * q : 4 * q + 4, :].bitcast(I32))
+            nc.scalar.dma_start(ws_raw[32 * q : 32 * q + 4, :].bitcast(I32), w1_scales[0, 4 * q : 4 * q + 4, :].bitcast(I32))
         nc.gpsimd.dma_start(gain[:], gn.rearrange("(p t) o -> p (t o)", t=PACK))
         nc.gpsimd.dma_start(w2_raw[:].bitcast(I32), w2_words[0].bitcast(I32))
         nc.scalar.activation(warm_out[:], warm[:], ACT.Relu)
@@ -77,8 +77,8 @@ def tile_picked_hashgaphinge_none_po_kernel(
             )
             return dealt
 
-        def deal_scales(name):
-            dealt = sb(name, [P, H], U8)
+        def deal_scales(name, tag=None):
+            dealt = sb(name, [P, H], U8, tag=tag)
             nc.vector.tensor_copy(
                 out=dealt[:].rearrange("p (t m) -> p t m", t=PACK),
                 in_=ws_raw[:].rearrange("p (m t) -> p t m", t=PACK),
@@ -87,9 +87,8 @@ def tile_picked_hashgaphinge_none_po_kernel(
 
         nc.vector.tensor_copy(xs_g[:], xs[:].indirect(offs_t[:]))
         for q in range(4):
-            queue = nc.scalar if q % 2 else nc.sync
-            queue.dma_start(xs_p[32 * q : 32 * q + 4, :].bitcast(I32), xs_g[32 * q : 32 * q + 32 : 8, :].bitcast(I32))
-        w1w = deal_words("w1w", w1_raw)
+            nc.scalar.dma_start(xs_p[32 * q : 32 * q + 4, :].bitcast(I32), xs_g[32 * q : 32 * q + 32 : 8, :].bitcast(I32))
+        w1w = deal_words("w1w", w1_raw, tag="xs")
         w1s = deal_scales("w1s")
         for q in range(4):
             nc.sync.dma_start(ws_raw[32 * q : 32 * q + 4, :].bitcast(I32), w2_scales[0, 4 * q : 4 * q + 4, :].bitcast(I32))
@@ -106,24 +105,23 @@ def tile_picked_hashgaphinge_none_po_kernel(
             )
 
         y = [sb("y%d" % t, [P, S], F32) for t in range(PACK)]
-        xq = []
-        for c, (j0, n) in enumerate(HALVES):
-            xq.append(sb("xq%d" % c, [P, n], U32))
-            nc.vector.tensor_copy(xq[c][:], xw[:].indirect(cut(offs_t, j0, n)))
+        xq = sb("xq", [P, S], U32, tag="w1_raw")
+        nc.vector.tensor_copy(xq[:], xw[:].indirect(offs_t[:]))
         for t in range(PACK):
             for c, (j0, n) in enumerate(HALVES):
                 acc = bank(4 * c + t, "y_acc%d_%d" % (c, t))
-                product(acc[:, :n], w1w, w1s, t, xq[c][:], xs_p[:, j0 : j0 + n])
+                product(acc[:, :n], w1w, w1s, t, xq[:, j0 : j0 + n], xs_p[:, j0 : j0 + n])
                 nc.scalar.activation(y[t][:, j0 : j0 + n], acc[:, :n], ACT.Copy, scale=gain[:, t : t + 1])
         w2w = deal_words("w2w", w2_raw, tag="xw")
-        w2s = deal_scales("w2s")
 
         def quantise(name, values, n, last, words, scales):
             grouped = sb(name, [P, n, PACK], BF16)
+            dst = grouped[:].rearrange("p (c i) t -> p c t i", i=4)
+            src = values[:].rearrange("p t (c i) -> p c t i", i=4)
             if last:
-                nc.vector.tensor_copy(out=grouped[:], in_=values[:].rearrange("p t j -> p j t"))
+                nc.vector.tensor_copy(out=dst, in_=src)
             else:
-                nc.scalar.copy(out=grouped[:], in_=values[:].rearrange("p t j -> p j t"))
+                nc.scalar.copy(out=dst, in_=src)
             nc.vector.quantize_mx(out=words.bitcast(FP8X4), scales=scales, in_=grouped[:].rearrange("p j t -> p (j t)"))
 
         h_pos = [sb("h_pos%d" % t, [P, S], F32) for t in range(PACK)]
@@ -135,11 +133,15 @@ def tile_picked_hashgaphinge_none_po_kernel(
                 if t < PACK:
                     if (c, t) == (2, 2):
                         subs.append(sb("sub%d_%d" % (c, t), [P, n], F32, tag="zb1"))
+                    elif (c, t) == (0, 1):
+                        subs.append(sb("sub%d_%d" % (c, t), [P, n], F32, tag="w2s"))
                     else:
                         subs.append(sb("sub%d_%d" % (c, t), [P, n], F32, tag="sub", bufs=2))
                     nc.vector.tensor_copy(subs[t][:], y[t][:].indirect(cut(n2_t, j0, n)))
                 if t > 0:
                     nc.vector.tensor_tensor(z[:, t - 1, :], y[t - 1][:].indirect(cut(n1_t, j0, n)), subs[t - 1][:], ALU.subtract)
+            if c == 0:
+                w2s = deal_scales("w2s")
             zw = sb("zw%d" % c, [P, n], U32)
             zs = sb("zs%d" % c, [P, n], U8)
             quantise("zb%d" % c, z, n, c == len(CHUNKS) - 1, zw[:], zs[:])

@@ -49,32 +49,30 @@ def tile_picked_hashgaphinge_none_po_kernel(
         w2_raw = sb("w2_raw", [P, 2 * N], U8)
         ws_raw = sb("ws_raw", [P, H], U8)
         gain = sb("gain", [P, PACK], F32)
-        warm = sb("warm", [P, 1], F32)
-        warm_out = sb("warm_out", [P, 1], F32)
 
-        nc.vector.memset(xs[:].bitcast(I32), 0)
+        nc.vector.memset(xs[:, : 3 * T // 4].bitcast(I32), 0)
+        nc.gpsimd.memset(xs[:, 3 * T // 4 :].bitcast(I32), 0)
         nc.gpsimd.memset(ws_raw[:].bitcast(I32), 0)
         nc.gpsimd.memset(xs_p[:].bitcast(I32), 0)
-        nc.gpsimd.memset(warm[:], 0.0)
 
         nc.sync.dma_start(offs_t[:], offs)
         nc.sync.dma_start(w1_raw[:].bitcast(I32), w1_words[0].bitcast(I32))
+        nc.sync.dma_start(xs[0:P:8, :].bitcast(I32), x_scales[0].bitcast(I32))
         nc.sync.dma_start(xw[:].bitcast(I32), x_words[0].rearrange("p n t -> p (n t)").bitcast(I32))
         for tile, src in ((n2_t, n2), (n1_t, n1), (n4_t, n4), (n3_t, n3)):
             nc.sync.dma_start(tile[:], src)
-        nc.scalar.dma_start(xs[0:P:8, :].bitcast(I32), x_scales[0].bitcast(I32))
         for q in range(4):
             nc.scalar.dma_start(ws_raw[32 * q : 32 * q + 4, :].bitcast(I32), w1_scales[0, 4 * q : 4 * q + 4, :].bitcast(I32))
         nc.gpsimd.dma_start(gain[:], gn.rearrange("(p t) o -> p (t o)", t=PACK))
         nc.gpsimd.dma_start(w2_raw[:].bitcast(I32), w2_words[0].bitcast(I32))
-        nc.scalar.activation(warm_out[:], warm[:], ACT.Relu)
 
-        def deal_words(name, raw, tag=None):
+        def deal_words(name, raw, parts, tag=None):
             dealt = sb(name, [P, 2 * H], U8, tag=tag)
-            nc.vector.tensor_copy(
-                out=dealt[:].rearrange("p (t m b) -> p t m b", t=PACK, b=2),
-                in_=raw[:].rearrange("p (m t b) -> p t m b", t=PACK, b=2),
-            )
+            dst = dealt[:].rearrange("p (t m b) -> p t m b", t=PACK, b=2)
+            src = raw[:].rearrange("p (m t b) -> p t m b", t=PACK, b=2)
+            step = PACK // parts
+            for t in range(0, PACK, step):
+                nc.vector.tensor_copy(out=dst[:, t : t + step], in_=src[:, t : t + step])
             return dealt
 
         def deal_scales(name, tag=None):
@@ -88,7 +86,7 @@ def tile_picked_hashgaphinge_none_po_kernel(
         nc.vector.tensor_copy(xs_g[:], xs[:].indirect(offs_t[:]))
         for q in range(4):
             nc.scalar.dma_start(xs_p[32 * q : 32 * q + 4, :].bitcast(I32), xs_g[32 * q : 32 * q + 32 : 8, :].bitcast(I32))
-        w1w = deal_words("w1w", w1_raw, tag="xs")
+        w1w = deal_words("w1w", w1_raw, 2)
         w1s = deal_scales("w1s")
         for q in range(4):
             nc.sync.dma_start(ws_raw[32 * q : 32 * q + 4, :].bitcast(I32), w2_scales[0, 4 * q : 4 * q + 4, :].bitcast(I32))
@@ -105,25 +103,30 @@ def tile_picked_hashgaphinge_none_po_kernel(
             )
 
         y = [sb("y%d" % t, [P, S], F32) for t in range(PACK)]
-        xq = sb("xq", [P, S], U32, tag="w1_raw")
+        xq = sb("xq", [P, S], U32, tag="xs")
         nc.vector.tensor_copy(xq[:], xw[:].indirect(offs_t[:]))
+        w2w = deal_words("w2w", w2_raw, 1, tag="xw")
         for t in range(PACK):
             for c, (j0, n) in enumerate(HALVES):
                 acc = bank(4 * c + t, "y_acc%d_%d" % (c, t))
                 product(acc[:, :n], w1w, w1s, t, xq[:, j0 : j0 + n], xs_p[:, j0 : j0 + n])
-                nc.scalar.activation(y[t][:, j0 : j0 + n], acc[:, :n], ACT.Copy, scale=gain[:, t : t + 1])
-        w2w = deal_words("w2w", w2_raw, tag="xw")
+                if (t, c) == (0, 1):
+                    nc.vector.tensor_scalar(y[t][:, j0 : j0 + n], acc[:, :n], gain[:, t : t + 1], None, ALU.mult)
+                else:
+                    nc.scalar.activation(y[t][:, j0 : j0 + n], acc[:, :n], ACT.Copy, scale=gain[:, t : t + 1])
 
-        def quantise(name, values, n, last, words, scales):
+        def quantise(name, values, n, on_vector, words, scales):
             grouped = sb(name, [P, n, PACK], BF16)
             dst = grouped[:].rearrange("p (c i) t -> p c t i", i=4)
-            src = values[:].rearrange("p t (c i) -> p c t i", i=4)
-            if last:
-                nc.vector.tensor_copy(out=dst, in_=src)
-            else:
-                nc.scalar.copy(out=dst, in_=src)
+            src = values.rearrange("p t (c i) -> p c t i", i=4)
+            split = on_vector // 4
+            if on_vector > 0:
+                nc.vector.tensor_copy(out=dst[:, :split], in_=src[:, :split])
+            if on_vector < n:
+                nc.scalar.copy(out=dst[:, split:], in_=src[:, split:])
             nc.vector.quantize_mx(out=words.bitcast(FP8X4), scales=scales, in_=grouped[:].rearrange("p j t -> p (j t)"))
 
+        h_acc = {}
         h_pos = [sb("h_pos%d" % t, [P, S], F32) for t in range(PACK)]
         h_neg = [sb("h_neg%d" % t, [P, S], F32) for t in range(PACK)]
         for c, (j0, n) in enumerate(CHUNKS):
@@ -131,9 +134,7 @@ def tile_picked_hashgaphinge_none_po_kernel(
             subs = []
             for t in range(PACK + 1):
                 if t < PACK:
-                    if (c, t) == (2, 2):
-                        subs.append(sb("sub%d_%d" % (c, t), [P, n], F32, tag="zb1"))
-                    elif (c, t) == (0, 1):
+                    if (c, t) == (0, 1):
                         subs.append(sb("sub%d_%d" % (c, t), [P, n], F32, tag="w2s"))
                     else:
                         subs.append(sb("sub%d_%d" % (c, t), [P, n], F32, tag="sub", bufs=2))
@@ -144,35 +145,46 @@ def tile_picked_hashgaphinge_none_po_kernel(
                 w2s = deal_scales("w2s")
             zw = sb("zw%d" % c, [P, n], U32)
             zs = sb("zs%d" % c, [P, n], U8)
-            quantise("zb%d" % c, z, n, c == len(CHUNKS) - 1, zw[:], zs[:])
+            quantise("zb%d" % c, z[:], n, n if c == len(CHUNKS) - 1 else 0, zw[:], zs[:])
             for t in range(PACK):
-                acc = bank(4 * (c % 2) + t, "h_acc%d_%d" % (c, t))
-                product(acc[:, :n], w2w, w2s, t, zw[:], zs[:])
-                nc.scalar.activation(h_pos[t][:, j0 : j0 + n], acc[:, :n], ACT.Copy)
-                nc.scalar.activation(h_neg[t][:, j0 : j0 + n], acc[:, :n], ACT.Copy, scale=-1.0)
+                if c < 2:
+                    h_acc[t] = bank(4 * c + t, "h_acc%d_%d" % (c, t))
+                product(h_acc[t][:, j0 % 256 : j0 % 256 + n], w2w, w2s, t, zw[:], zs[:])
+                if c != 1:
+                    half = slice(256 * (c // 2), 256 * (c // 2) + 256)
+                    nc.scalar.activation(h_pos[t][:, half], h_acc[t][:, :256], ACT.Copy)
+                    nc.scalar.activation(h_neg[t][:, half], h_acc[t][:, :256], ACT.Copy, scale=-1.0)
 
         out_rows = out_0.rearrange("(p t) j -> p t j", t=PACK)
         out_words = out_1[0].rearrange("p j t -> p (j t)").bitcast(I32)
         os_all = sb("os_all", [P, S], U8)
-        for c, (j0, n) in enumerate(CHUNKS):
-            up = sb("up%d" % c, [P, PACK, n], F32)
-            half_up = sb("half_up%d" % c, [P, PACK, n], F32)
-            downs = []
-            res = sb("res%d" % c, [P, PACK, n], F32)
-            for t in range(PACK + 1):
-                if t < PACK:
-                    nc.vector.tensor_tensor(up[:, t, :], h_pos[t][:].indirect(cut(n4_t, j0, n)), h_neg[t][:, j0 : j0 + n], ALU.add)
-                    nc.scalar.activation(half_up[:, t, :], up[:, t, :], ACT.Relu, scale=0.5)
-                    downs.append(sb("down%d_%d" % (c, t), [P, n], F32, tag="down", bufs=2))
-                    nc.vector.tensor_tensor(downs[t][:], h_neg[t][:].indirect(cut(n3_t, j0, n)), h_pos[t][:, j0 : j0 + n], ALU.add)
-                if t > 0:
-                    nc.vector.scalar_tensor_tensor(
-                        out=res[:, t - 1, :], in0=downs[t - 1][:], scalar=0.0, in1=half_up[:, t - 1, :], op0=ALU.max, op1=ALU.add
-                    )
-            ow = sb("ow%d" % c, [P, n], U32)
-            quantise("ob%d" % c, res, n, c == len(CHUNKS) - 1, ow[:], os_all[:, j0 : j0 + n])
-            nc.sync.dma_start(out_rows[:, :, j0 : j0 + n], res[:])
-            nc.sync.dma_start(out_words[:, j0 : j0 + n], ow[:].bitcast(I32))
+        res = [sb("res%d" % c, [P, PACK, n], F32) for c, (j0, n) in enumerate(HALVES)]
+        steps = [(t, j0, n) for j0, n in HALVES for t in range(PACK)][:-1] + [(PACK - 1, j0, n) for j0, n in CHUNKS[1:]]
+        waiting = None
+        for step in steps + [None]:
+            ready = waiting
+            if step is not None:
+                t, j0, n = step
+                up = sb("up%d_%d" % (t, j0), [P, n], F32)
+                half_up = sb("half_up%d_%d" % (t, j0), [P, n], F32)
+                down = sb("down%d_%d" % (t, j0), [P, n], F32, tag="down", bufs=3)
+                nc.vector.tensor_tensor(up[:], h_pos[t][:].indirect(cut(n4_t, j0, n)), h_neg[t][:, j0 : j0 + n], ALU.add)
+                nc.scalar.activation(half_up[:], up[:], ACT.Relu, scale=0.5)
+                nc.vector.tensor_tensor(down[:], h_neg[t][:].indirect(cut(n3_t, j0, n)), h_pos[t][:, j0 : j0 + n], ALU.add)
+                waiting = (t, j0, n, down, half_up)
+            if ready is not None:
+                t, j0, n, down, half_up = ready
+                part = res[j0 // 256][:, :, j0 % 256 : j0 % 256 + n]
+                nc.vector.scalar_tensor_tensor(out=part[:, t, :], in0=down[:], scalar=0.0, in1=half_up[:], op0=ALU.max, op1=ALU.add)
+                if j0 >= 256:
+                    nc.sync.dma_start(out_rows[:, t, j0 : j0 + n], part[:, t, :])
+                if t == PACK - 1:
+                    ow = sb("ow%d" % j0, [P, n], U32)
+                    quantise("ob%d" % j0, part, n, n if step is None else 0, ow[:], os_all[:, j0 : j0 + n])
+                    if j0 < 256:
+                        nc.sync.dma_start(out_rows[:, :, j0 : j0 + n], part)
+                    queue = nc.scalar if step is None else nc.sync
+                    queue.dma_start(out_words[:, j0 : j0 + n], ow[:].bitcast(I32))
         for q in range(4):
             queue = nc.scalar if q % 2 else nc.sync
             queue.dma_start(out_2[0, 4 * q : 4 * q + 4, :].bitcast(I32), os_all[32 * q : 32 * q + 4, :].bitcast(I32))

from contextlib import ExitStack

import concourse.mybir as mybir

K, T, S, H, N = 512, 2048, 512, 512, 512
FLOPS = 2 * K * H * S + 2 * H * N * S

F32 = mybir.dt.float32
BF16 = mybir.dt.bfloat16
I32 = mybir.dt.int32
U32 = mybir.dt.uint32
U16 = mybir.dt.uint16
U8 = mybir.dt.uint8
FP8X4 = mybir.dt.float8_e4m3fn_x4
FP4X4 = mybir.dt.float4_e2m1fn_x4
ALU = mybir.AluOpType
ACT = mybir.ActivationFunctionType

P = 128
PACK = 4
HALVES = [(0, 256), (256, 256)]
CHUNKS = [(0, 256), (256, 128), (384, 128)]


def tile_picked_hashgaphinge_none_po_kernel(
    tc, x_words, x_scales, w1_words, w1_scales, gn, w2_words, w2_scales, offs, n1, n2, n3, n4, out_0, out_1, out_2
):
    nc = tc.nc
    with ExitStack() as ctx:
        pool = ctx.enter_context(tc.tile_pool(name="pool", bufs=1))
        psum = ctx.enter_context(tc.psum_pool(name="psum", bufs=1))

        def sb(name, shape, dtype, tag=None, bufs=1):
            return pool.tile(shape, dtype, name=name, tag=tag or name, bufs=bufs, align_bytes=64)

        def bank(index, name):
            return psum.tile([P, 512], F32, name=name, tag="bank%d" % index)

        def cut(lists, j0, n):
            return lists[:, j0 // 16 : (j0 + n) // 16]

        lists = [sb(name, [P, S // 16], U16) for name in ("offs_t", "n1_t", "n2_t", "n3_t", "n4_t")]
        offs_t, n1_t, n2_t, n3_t, n4_t = lists
        xw = sb("xw", [P, T], U32)
        xs = sb("xs", [P, T], U8)
        xs_g = sb("xs_g", [P, S], U8)
        xs_p = sb("xs_p", [P, S], U8)
        w1_raw = sb("w1_raw", [P, 2 * H], U8)
        w2_raw = sb("w2_raw", [P, 2 * N], U8)
        ws_raw = sb("ws_raw", [P, H], U8)
        gain = sb("gain", [P, PACK], F32)

        nc.vector.memset(xs[:, : 3 * T // 4].bitcast(I32), 0)
        nc.gpsimd.memset(xs[:, 3 * T // 4 :].bitcast(I32), 0)
        nc.gpsimd.memset(ws_raw[:].bitcast(I32), 0)
        nc.gpsimd.memset(xs_p[:].bitcast(I32), 0)

        nc.sync.dma_start(offs_t[:], offs)
        nc.sync.dma_start(w1_raw[:].bitcast(I32), w1_words[0].bitcast(I32))
        nc.sync.dma_start(xs[0:P:8, :].bitcast(I32), x_scales[0].bitcast(I32))
        nc.sync.dma_start(xw[:].bitcast(I32), x_words[0].rearrange("p n t -> p (n t)").bitcast(I32))
        for tile, src in ((n2_t, n2), (n1_t, n1), (n4_t, n4), (n3_t, n3)):
            nc.sync.dma_start(tile[:], src)
        for q in range(4):
            nc.scalar.dma_start(ws_raw[32 * q : 32 * q + 4, :].bitcast(I32), w1_scales[0, 4 * q : 4 * q + 4, :].bitcast(I32))
        nc.gpsimd.dma_start(gain[:], gn.rearrange("(p t) o -> p (t o)", t=PACK))
        nc.gpsimd.dma_start(w2_raw[:].bitcast(I32), w2_words[0].bitcast(I32))

        def deal_words(name, raw, parts, tag=None):
            dealt = sb(name, [P, 2 * H], U8, tag=tag)
            dst = dealt[:].rearrange("p (t m b) -> p t m b", t=PACK, b=2)
            src = raw[:].rearrange("p (m t b) -> p t m b", t=PACK, b=2)
            step = PACK // parts
            for t in range(0, PACK, step):
                nc.vector.tensor_copy(out=dst[:, t : t + step], in_=src[:, t : t + step])
            return dealt

        def deal_scales(name, tag=None):
            dealt = sb(name, [P, H], U8, tag=tag)
            nc.vector.tensor_copy(
                out=dealt[:].rearrange("p (t m) -> p t m", t=PACK),
                in_=ws_raw[:].rearrange("p (m t) -> p t m", t=PACK),
            )
            return dealt

        nc.vector.tensor_copy(xs_g[:], xs[:].indirect(offs_t[:]))
        for q in range(4):
            nc.scalar.dma_start(xs_p[32 * q : 32 * q + 4, :].bitcast(I32), xs_g[32 * q : 32 * q + 32 : 8, :].bitcast(I32))
        w1w = deal_words("w1w", w1_raw, 2)
        w1s = deal_scales("w1s")
        for q in range(4):
            nc.sync.dma_start(ws_raw[32 * q : 32 * q + 4, :].bitcast(I32), w2_scales[0, 4 * q : 4 * q + 4, :].bitcast(I32))

        def product(out, words, scales, t, rhs, rhs_scale):
            nc.tensor.matmul_mx(
                out=out,
                lhsT=words[:, 2 * P * t : 2 * P * (t + 1)].bitcast(FP4X4),
                lhsT_scale=scales[:, P * t : P * (t + 1)],
                rhs=rhs.bitcast(FP8X4),
                rhs_scale=rhs_scale,
                start=True,
                stop=True,
            )

        y = [sb("y%d" % t, [P, S], F32) for t in range(PACK)]
        xq = sb("xq", [P, S], U32, tag="xs")
        nc.vector.tensor_copy(xq[:], xw[:].indirect(offs_t[:]))
        w2w = deal_words("w2w", w2_raw, 1, tag="xw")
        for t in range(PACK):
            for c, (j0, n) in enumerate(HALVES):
                acc = bank(4 * c + t, "y_acc%d_%d" % (c, t))
                product(acc[:, :n], w1w, w1s, t, xq[:, j0 : j0 + n], xs_p[:, j0 : j0 + n])
                if (t, c) == (0, 1):
                    nc.vector.tensor_scalar(y[t][:, j0 : j0 + n], acc[:, :n], gain[:, t : t + 1], None, ALU.mult)
                else:
                    nc.scalar.activation(y[t][:, j0 : j0 + n], acc[:, :n], ACT.Copy, scale=gain[:, t : t + 1])

        def quantise(name, values, n, on_vector, words, scales):
            grouped = sb(name, [P, n, PACK], BF16)
            dst = grouped[:].rearrange("p (c i) t -> p c t i", i=4)
            src = values.rearrange("p t (c i) -> p c t i", i=4)
            split = on_vector // 4
            if on_vector > 0:
                nc.vector.tensor_copy(out=dst[:, :split], in_=src[:, :split])
            if on_vector < n:
                nc.scalar.copy(out=dst[:, split:], in_=src[:, split:])
            nc.vector.quantize_mx(out=words.bitcast(FP8X4), scales=scales, in_=grouped[:].rearrange("p j t -> p (j t)"))

        h_acc = {}
        h_pos = [sb("h_pos%d" % t, [P, S], F32) for t in range(PACK)]
        h_neg = [sb("h_neg%d" % t, [P, S], F32) for t in range(PACK)]
        for c, (j0, n) in enumerate(CHUNKS):
            z = sb("z%d" % c, [P, PACK, n], F32, tag="zb0" if c == 2 else None)
            subs = []
            for t in range(PACK + 1):
                if t < PACK:
                    if (c, t) == (0, 1):
                        subs.append(sb("sub%d_%d" % (c, t), [P, n], F32, tag="w2s"))
                    else:
                        subs.append(sb("sub%d_%d" % (c, t), [P, n], F32, tag="sub", bufs=2))
                    nc.vector.tensor_copy(subs[t][:], y[t][:].indirect(cut(n2_t, j0, n)))
                if t > 0:
                    nc.vector.tensor_tensor(z[:, t - 1, :], y[t - 1][:].indirect(cut(n1_t, j0, n)), subs[t - 1][:], ALU.subtract)
            if c == 0:
                w2s = deal_scales("w2s")
            zw = sb("zw%d" % c, [P, n], U32)
            zs = sb("zs%d" % c, [P, n], U8)
            quantise("zb%d" % c, z[:], n, n if c == len(CHUNKS) - 1 else 0, zw[:], zs[:])
            for t in range(PACK):
                if c < 2:
                    h_acc[t] = bank(4 * c + t, "h_acc%d_%d" % (c, t))
                product(h_acc[t][:, j0 % 256 : j0 % 256 + n], w2w, w2s, t, zw[:], zs[:])
                if c != 1:
                    half = slice(256 * (c // 2), 256 * (c // 2) + 256)
                    nc.scalar.activation(h_pos[t][:, half], h_acc[t][:, :256], ACT.Copy)
                    nc.scalar.activation(h_neg[t][:, half], h_acc[t][:, :256], ACT.Copy, scale=-1.0)

        out_rows = out_0.rearrange("(p t) j -> p t j", t=PACK)
        out_words = out_1[0].rearrange("p j t -> p (j t)").bitcast(I32)
        os_all = sb("os_all", [P, S], U8)
        res = [sb("res%d" % c, [P, PACK, n], F32) for c, (j0, n) in enumerate(HALVES)]
        steps = [(t, j0, n) for j0, n in HALVES for t in range(PACK)][:-1] + [(PACK - 1, j0, n) for j0, n in CHUNKS[1:]]
        waiting = None
        for step in steps + [None]:
            ready = waiting
            if step is not None:
                t, j0, n = step
                up = sb("up%d_%d" % (t, j0), [P, n], F32)
                half_up = sb("half_up%d_%d" % (t, j0), [P, n], F32)
                down = sb("down%d_%d" % (t, j0), [P, n], F32, tag="down", bufs=3)
                nc.vector.tensor_tensor(up[:], h_pos[t][:].indirect(cut(n4_t, j0, n)), h_neg[t][:, j0 : j0 + n], ALU.add)
                nc.scalar.activation(half_up[:], up[:], ACT.Relu, scale=0.5)
                nc.vector.tensor_tensor(down[:], h_neg[t][:].indirect(cut(n3_t, j0, n)), h_pos[t][:, j0 : j0 + n], ALU.add)
                waiting = (t, j0, n, down, half_up)
            if ready is not None:
                t, j0, n, down, half_up = ready
                part = res[j0 // 256][:, :, j0 % 256 : j0 % 256 + n]
                nc.vector.scalar_tensor_tensor(out=part[:, t, :], in0=down[:], scalar=0.0, in1=half_up[:], op0=ALU.max, op1=ALU.add)
                if j0 >= 256:
                    nc.sync.dma_start(out_rows[:, t, j0 : j0 + n], part[:, t, :])
                if t == PACK - 1:
                    ow = sb("ow%d" % j0, [P, n], U32)
                    quantise("ob%d" % j0, part, n, n if step is None else 0, ow[:], os_all[:, j0 : j0 + n])
                    if j0 < 256:
                        nc.sync.dma_start(out_rows[:, :, j0 : j0 + n], part)
                    queue = nc.scalar if step is None else nc.sync
                    queue.dma_start(out_words[:, j0 : j0 + n], ow[:].bitcast(I32))
        for q in range(4):
            queue = nc.scalar if q % 2 else nc.sync
            queue.dma_start(out_2[0, 4 * q : 4 * q + 4, :].bitcast(I32), os_all[32 * q : 32 * q + 4, :].bitcast(I32))
